import numpy as np
import ml_dtypes


def mxq(x, axis, fmt="e4m3"):
    dtype, down = {"e4m3": (ml_dtypes.float8_e4m3fn, 7), "e5m2": (ml_dtypes.float8_e5m2, 14)}[fmt]
    v = np.moveaxis(np.asarray(x, np.float32).astype(ml_dtypes.bfloat16).astype(np.float64), axis, -1)
    blocks = v.reshape(v.shape[:-1] + (-1, 32))
    amax = np.abs(blocks).max(-1, keepdims=True)
    byte = np.maximum(np.where(amax > 0, np.frexp(amax)[1] - 1 + 127, 0) - down, 1)
    scale = np.exp2(byte - 127.0)
    codes = (blocks / scale).astype(np.float32).astype(dtype).astype(np.float64)
    return np.moveaxis((codes * scale).reshape(v.shape), -1, axis)


WIDE = False


def mx_kscale(k):
    if not WIDE:
        return np.ones(k)
    levels = np.array([10, -10, 5, -5, 0])
    if k % 512:
        return np.exp2(np.random.permutation(np.resize(levels, k // 32))).repeat(32)
    a = np.empty((k // 512, 16))
    for p in range(k // 512):
        a[p, :8] = np.random.permutation(np.resize(levels, 8))
        for g in range(8):
            far = levels[np.abs(levels - a[p, g]) >= 10]
            a[p, g + 8] = far[np.random.randint(len(far))]
    return np.exp2(a.ravel()).repeat(32)


def f64(x):
    return np.asarray(x).astype(np.float64)


def striped(idx):
    return np.tile(idx.reshape(-1, 16).T, (8, 1)).astype(np.uint16)


def unstriped(offs):
    return offs[:16].T.reshape(-1).astype(np.int64)


def striped8(idx):
    return np.concatenate([x.reshape(-1, 16).T for x in idx]).astype(np.uint16)


def runs(offs, k):
    lists = np.stack([offs[16 * r : 16 * r + 16].T.reshape(-1) for r in range(8)]).astype(np.int64)
    return lists[np.arange(k) % 512 // 64]


def pack_weight(w):
    k, n = w.shape
    w = f64(np.asarray(w, np.float32).astype(ml_dtypes.bfloat16)).reshape(k // 32, 32, n)
    amax = np.abs(w).max(1)
    byte = np.clip(np.where(amax > 0, np.frexp(amax)[1] - 1 + 127 - 7, 1), 1, 254)
    scaled = (w * np.exp2(127.0 - byte)[:, None, :]).reshape(k, n).astype(np.float32)
    words = np.ascontiguousarray(scaled.reshape(k // 512, 128, 4, n).transpose(0, 1, 3, 2)).astype(ml_dtypes.float8_e4m3fn).view(np.uint8)
    return words, np.ascontiguousarray(byte.astype(np.uint8).reshape(k // 512, 16, n))


def unpack_weight(words, scales):
    g, p, n, _ = words.shape
    vals = np.ascontiguousarray(words).view(ml_dtypes.float8_e4m3fn).astype(np.float64) * np.repeat(np.exp2(scales.astype(np.float64) - 127.0), 8, axis=1)[..., None]
    return vals.transpose(0, 1, 3, 2).reshape(g * 512, n)


def sigmoid(v):
    return 1.0 / (1.0 + np.exp(-np.maximum(v, -700.0)))

def planes(y):
    n, m = y.shape
    v = y.astype(np.float32).astype(ml_dtypes.bfloat16).astype(np.float64).reshape(n // 32, 32, m)
    top = np.abs(v).max(1)
    byte = np.clip(np.where(top > 0, np.frexp(top)[1] - 1 + 127 - 7, 1), 1, 254)
    codes = (v * np.exp2(127.0 - byte)[:, None, :]).reshape(n, m).astype(np.float32).astype(ml_dtypes.float8_e4m3fn).view(np.uint8)
    words = codes.reshape(n // 512, 128, 4, m).transpose(0, 1, 3, 2)
    return np.ascontiguousarray(words), np.ascontiguousarray(byte.astype(np.uint8).reshape(n // 512, 16, m))


K, T, S, V, H, J = 512, 2048, 512, 512, 512, 512


def setup_inputs():
    n = np.random.standard_normal
    s = mx_kscale(K)[:, None]
    u = mx_kscale(S)
    packed_xT = pack_weight(n((K, T)) * s)
    packed_w1 = pack_weight(n((K, H)) / np.sqrt(K) / s)
    packed_w2 = pack_weight(n((K, H)) / np.sqrt(K) / s)
    return {
        "x_words": packed_xT[0],
        "x_scales": packed_xT[1],
        "w1_words": packed_w1[0],
        "w1_scales": packed_w1[1],
        "w2_words": packed_w2[0],
        "w2_scales": packed_w2[1],
        "ga": (np.random.uniform(0.5, 1.5, (H, 1)) * u[:, None]).astype(np.float32),
        "gb": (np.random.uniform(0.5, 1.5, (H, 1)) / u[:, None]).astype(np.float32),
        "tab": n((S, J)).astype(np.float32),
        "offs": striped(np.random.permutation(T)[:S]),
        "two": striped(np.random.permutation(T)[:V]),
        "n1": striped8(np.stack([np.random.permutation(S) for _ in range(8)])),
        "n2": striped8(np.stack([np.random.permutation(S) for _ in range(8)])),
        "n3": striped8(np.stack([np.random.permutation(V) for _ in range(8)])),
        "n4": striped8(np.random.randint(0, J, (8, V))),
        "n5": striped8(np.stack([np.random.permutation(V) for _ in range(8)])),
    }


def reference(x_words, x_scales, w1_words, w1_scales, w2_words, w2_scales, ga, gb, tab, offs, two, n1, n2, n3, n4, n5):
    xq = unpack_weight(x_words, x_scales)[:, unstriped(offs)]
    a = unpack_weight(w1_words, w1_scales).T @ xq
    pa = a[np.arange(H)[:, None], runs(n1, H)]
    pb = a[np.arange(H)[:, None], runs(n2, H)]
    mu = 0.3125 * (a + pa + pb)
    z = f64(ga) * ((a - mu) / (np.sqrt((pa - mu) ** 2 + (pb - mu) ** 2 + 0.25)))
    x_two = unpack_weight(x_words, x_scales)[:, unstriped(two)]
    b = unpack_weight(w2_words, w2_scales).T @ x_two
    st = b * (sigmoid(b[np.arange(H)[:, None], runs(n3, H)]))
    z2 = f64(gb) * (np.maximum(st, st[np.arange(H)[:, None], runs(n3, H)]))
    s = 0.0625 * ((mxq(z, 0, "e4m3").T @ mxq(z2, 0, "e4m3")))
    out_0 = np.maximum(s + f64(tab)[np.arange(S)[:, None], runs(n4, S)], s[np.arange(S)[:, None], runs(n5, S)])
    return (out_0,) + planes(out_0)

@@ -1,0 +1,253 @@
+from contextlib import ExitStack
+
+import concourse.mybir as mybir
+from concourse.masks import make_identity
+
+F32 = mybir.dt.float32
+BF16 = mybir.dt.bfloat16
+I32 = mybir.dt.int32
+U32 = mybir.dt.uint32
+U16 = mybir.dt.uint16
+U8 = mybir.dt.uint8
+FP8X4 = mybir.dt.float8_e4m3fn_x4
+ALU = mybir.AluOpType
+ACT = mybir.ActivationFunctionType
+
+P = 128
+PACK = 4
+T = 2048
+N = 512
+C = 0.3125
+CHUNKS = (256, 128, 128)
+FLOPS = 3 * 2 * 512 * 512 * 512
+
+
+def tile_picked_kqstdtwicpkind_none_po_kernel(
+    tc, x_words, x_scales, w1_words, w1_scales, w2_words, w2_scales, ga, gb, tab,
+    offs, two, n1, n2, n3, n4, n5, out_0, out_1, out_2,
+):
+    nc = tc.nc
+    with ExitStack() as ctx:
+        keep = ctx.enter_context(tc.tile_pool(name="keep", bufs=1))
+        ring = ctx.enter_context(tc.tile_pool(name="ring", bufs=2))
+        psum = ctx.enter_context(tc.psum_pool(name="psum", bufs=8))
+
+        def held(shape, dtype, name):
+            return keep.tile(shape, dtype, name=name, align_bytes=64)
+
+        def bank():
+            return psum.tile([P, N], F32, name="bank")
+
+        def load_list(src, name):
+            tile = keep.tile([P, N // 16], U16, name=name)
+            nc.sync.dma_start(tile[:], src)
+            return tile
+
+        def words_of(src):
+            return src[0].rearrange("p n r -> p (n r)").bitcast(I32)
+
+        def load_scale_rows(tile, first, src, quadrants):
+            for q in quadrants:
+                nc.sync.dma_start(
+                    tile[32 * q + first : 32 * q + first + 4, :].bitcast(I32),
+                    src[0, 4 * q : 4 * q + 4, :].bitcast(I32),
+                )
+
+        x_sc = held([P, T], U8, "x_sc")
+        w_sc_raw = held([P, N], U8, "w_sc_raw")
+        nc.gpsimd.memset(x_sc[:].bitcast(I32), 0)
+        nc.gpsimd.memset(w_sc_raw[:].bitcast(I32), 0)
+        warm = held([P, 1], F32, "warm")
+        nc.vector.memset(warm[:], 0.0)
+        warm_out = held([P, 1], F32, "warm_out")
+        nc.scalar.activation(warm_out[:], warm[:], ACT.Sigmoid)
+
+        load_scale_rows(x_sc, 0, x_scales, range(4))
+        offs_t = load_list(offs, "offs_t")
+        load_scale_rows(w_sc_raw, 0, w1_scales, range(1))
+        w1_raw = held([P, N], U32, "w1_raw")
+        nc.sync.dma_start(w1_raw[:].bitcast(I32), words_of(w1_words))
+        x_w = held([P, T], U32, "x_w")
+        nc.sync.dma_start(x_w[:].bitcast(I32), words_of(x_words))
+        load_scale_rows(w_sc_raw, 0, w1_scales, range(1, 4))
+        load_scale_rows(w_sc_raw, 4, w2_scales, range(4))
+        two_t = load_list(two, "two_t")
+        n1_t = load_list(n1, "n1_t")
+        n2_t = load_list(n2, "n2_t")
+        w2_raw = held([P, N], U32, "w2_raw")
+        nc.sync.dma_start(w2_raw[:].bitcast(I32), words_of(w2_words))
+        n3_t = load_list(n3, "n3_t")
+        ga_t = held([P, PACK], F32, "ga_t")
+        gb_t = held([P, PACK], F32, "gb_t")
+        nc.sync.dma_start(ga_t[:], ga.rearrange("(p t) o -> p (t o)", t=PACK))
+        nc.sync.dma_start(gb_t[:], gb.rearrange("(p t) o -> p (t o)", t=PACK))
+        n4_t = load_list(n4, "n4_t")
+        n5_t = load_list(n5, "n5_t")
+        tab_rows = tab.rearrange("(p t) j -> p t j", t=PACK)
+        tab_t = []
+        for t in range(PACK):
+            tab_t.append(held([P, N], F32, "tab%d" % t))
+            nc.sync.dma_start(tab_t[t][:, 0:N], tab_rows[:, t, :])
+
+        ident = held([P, P], F32, "ident")
+        make_identity(nc, ident[:])
+
+        sign = held([P, PACK], F32, "sign")
+        half = held([P, PACK], F32, "half")
+        gb_abs = held([P, PACK], F32, "gb_abs")
+        ga_signed = held([P, PACK], F32, "ga_signed")
+        sign_c = held([P, PACK], F32, "sign_c")
+        nc.gpsimd.tensor_scalar(half[:], gb_t[:], 0.0, 2.0, ALU.is_ge, ALU.mult)
+        nc.gpsimd.tensor_scalar(sign[:], half[:], 1.0, -1.0, ALU.mult, ALU.add)
+        nc.gpsimd.tensor_scalar(sign_c[:], half[:], C, -C, ALU.mult, ALU.add)
+        nc.gpsimd.tensor_tensor(gb_abs[:], gb_t[:], sign[:], ALU.mult)
+        nc.gpsimd.tensor_tensor(ga_signed[:], ga_t[:], sign_c[:], ALU.mult)
+
+        def deal(dst, src):
+            nc.vector.tensor_copy(
+                dst.rearrange("p (t m) -> p m t", t=PACK), src.rearrange("p (m t) -> p m t", t=PACK)
+            )
+
+        def pick(src, lst, dtype, name):
+            tile = held([P, N], dtype, name)
+            nc.vector.tensor_copy(tile[:], src[:].indirect(lst[:]))
+            return tile
+
+        xa_sc = pick(x_sc, offs_t, U8, "xa_sc")
+        xb_sc = pick(x_sc, two_t, U8, "xb_sc")
+        w1_d = held([P, N], U32, "w1_d")
+        w2_d = held([P, N], U32, "w2_d")
+        w_sc = held([P, N], U8, "w_sc")
+        deal(w1_d[:].bitcast(I32), w1_raw[:].bitcast(I32))
+        deal(w_sc[:], w_sc_raw[:])
+        xa_w = pick(x_w, offs_t, U32, "xa_w")
+        xb_w = pick(x_w, two_t, U32, "xb_w")
+        deal(w2_d[:].bitcast(I32), w2_raw[:].bitcast(I32))
+
+        def product(lhs_w, lhs_sc, first, t, rhs_w, rhs_sc):
+            acc = bank()
+            cols = slice(P * t, P * (t + 1))
+            nc.tensor.matmul_mx(
+                out=acc[:], lhsT=lhs_w[:, cols].bitcast(FP8X4), lhsT_scale=lhs_sc[first:P, cols],
+                rhs=rhs_w[:].bitcast(FP8X4), rhs_scale=rhs_sc[:], start=True, stop=True,
+            )
+            return acc
+
+        a_win, b_win, neg_win = [], [], []
+        for t in range(PACK):
+            acc = product(w1_d, w_sc, 0, t, xa_w, xa_sc)
+            a_win.append(held([P, 2 * N], F32, "a_win%d" % t))
+            nc.scalar.copy(a_win[t][:, 0:N], acc[:])
+            nc.scalar.activation(a_win[t][:, N : 2 * N], acc[:], ACT.Copy, scale=5.0 / 3.0)
+        for t in range(PACK):
+            acc = product(w2_d, w_sc, 4, t, xb_w, xb_sc)
+            b_win.append(held([P, 2 * N], F32, "b_win%d" % t))
+            nc.scalar.copy(b_win[t][:, 0:N], acc[:])
+        gates = []
+        for t in range(PACK):
+            gates.append(held([P, N], F32, "gate%d" % t))
+            nc.scalar.activation(gates[t][:], b_win[t][:].indirect(n3_t[:]), ACT.Sigmoid)
+
+        def turned_sum(terms):
+            acc = bank()
+            for k in range(N // P):
+                cols = slice(P * k, P * (k + 1))
+                for i, term in enumerate(terms):
+                    nc.tensor.matmul(
+                        acc[:, cols], lhsT=term[:, cols], rhs=ident[:], is_transpose=True,
+                        start=(i == 0), stop=(i == len(terms) - 1),
+                    )
+            return acc
+
+        centred, squares = [], []
+        for t in range(PACK):
+            a = a_win[t][:, 0:N]
+            pa = ring.tile([P, N], F32, name="pa")
+            neg_sum = ring.tile([P, N], F32, name="neg_sum")
+            nc.vector.tensor_copy(pa[:], a_win[t][:].indirect(n1_t[:]))
+            pb = ring.tile([P, N], F32, name="pb")
+            nc.vector.tensor_copy(pb[:], a_win[t][:].indirect(n2_t[:]))
+            nc.vector.scalar_tensor_tensor(neg_sum[:], pa[:], -1.0, pb[:], ALU.mult, ALU.subtract)
+            centred.append(held([P, N], F32, "centred%d" % t))
+            nc.vector.scalar_tensor_tensor(centred[t][:], a, 2.2, neg_sum[:], ALU.mult, ALU.add)
+            diff = turned_sum([pa[:], pa[:], neg_sum[:]])
+            mean = turned_sum([neg_sum[:], a_win[t][:, N : 2 * N]])
+            sq = held([P, 2, N], F32, "sq%d" % t)
+            nc.scalar.activation(sq[:, 0, :], diff[:], ACT.Square)
+            nc.scalar.activation(sq[:, 1, :], mean[:], ACT.Square, scale=0.375)
+            squares.append(sq)
+        inv_root = []
+        for t in range(PACK):
+            total = turned_sum([squares[t][:, 0, :], squares[t][:, 1, :]])
+            inv_root.append(held([P, N], F32, "inv_root%d" % t))
+            nc.scalar.activation(inv_root[t][:], total[:], ACT.Abs_reciprocal_sqrt, scale=0.5, bias=0.25)
+
+        looked = held([P, PACK, N], F32, "looked")
+        z2_planes = held([P, PACK, N], BF16, "z2_planes")
+        for t in range(PACK):
+            st = a_win[t][:, 0:N]
+            nc.vector.scalar_tensor_tensor(
+                st, b_win[t][:, 0:N], gb_abs[:, t : t + 1], gates[t][:], ALU.mult, ALU.mult
+            )
+            nc.vector.tensor_copy(looked[:, t, :], a_win[t][:].indirect(n3_t[:]))
+            nc.vector.tensor_tensor(z2_planes[:, t, :], st, looked[:, t, :], ALU.max)
+        z2_il = held([P, N * PACK], BF16, "z2_il")
+        nc.scalar.copy(
+            z2_il[:].rearrange("p (c i t) -> p c t i", i=4, t=PACK),
+            z2_planes[:].rearrange("p t (c i) -> p c t i", i=4),
+        )
+        z2_w = held([P, N], U32, "z2_w")
+        z2_sc = held([P, N], U8, "z2_sc")
+        nc.vector.quantize_mx(out=z2_w[:].bitcast(FP8X4), scales=z2_sc[:], in_=z2_il[:])
+
+        z_planes = held([P, PACK, N], BF16, "z_planes")
+        for t in range(PACK):
+            nc.vector.scalar_tensor_tensor(
+                z_planes[:, t, :], centred[t][:], ga_signed[:, t : t + 1], inv_root[t][:], ALU.mult, ALU.mult
+            )
+        z_il = held([P, N * PACK], BF16, "z_il")
+        nc.scalar.copy(
+            z_il[:].rearrange("p (u m t) -> p m t u", u=PACK, t=PACK),
+            z_planes[:].rearrange("p t (m u) -> p m t u", u=PACK),
+        )
+        z_w = held([P, N], U32, "z_w")
+        z_sc = held([P, N], U8, "z_sc")
+        for t in range(PACK):
+            for h in range(2):
+                nc.vector.tensor_copy(
+                    looked[:, t, 256 * h : 256 * (h + 1)], tab_t[t][:].indirect(n4_t[:, 16 * h : 16 * (h + 1)])
+                )
+        nc.vector.quantize_mx(out=z_w[:].bitcast(FP8X4), scales=z_sc[:], in_=z_il[:])
+
+        s_win = []
+        with_tab = held([P, PACK, N], F32, "with_tab")
+        for t in range(PACK):
+            acc = product(z_w, z_sc, 0, t, z2_w, z2_sc)
+            s_win.append(held([P, N], F32, "s_win%d" % t))
+            nc.scalar.activation(s_win[t][:], acc[:], ACT.Copy, scale=0.0625)
+            nc.vector.scalar_tensor_tensor(with_tab[:, t, :], acc[:], 0.0625, looked[:, t, :], ALU.mult, ALU.add)
+
+        out_rows = out_0.rearrange("(p t) v -> p t v", t=PACK)
+        out_w = held([P, N], U32, "out_w")
+        out_sc = held([P, N], U8, "out_sc")
+        c0 = 0
+        for k, width in enumerate(CHUNKS):
+            cols = slice(c0, c0 + width)
+            other = held([P, PACK, width], F32, "other%d" % k)
+            for t in range(PACK):
+                nc.vector.tensor_copy(other[:, t, :], s_win[t][:].indirect(n5_t[:, c0 // 16 : (c0 + width) // 16]))
+            res = held([P, PACK, width], F32, "res%d" % k)
+            nc.vector.tensor_tensor(res[:], with_tab[:, :, cols], other[:], ALU.max)
+            nc.sync.dma_start(out_rows[:, :, cols], res[:])
+            res_il = held([P, width * PACK], BF16, "res_il%d" % k)
+            copy = nc.vector.tensor_copy if k == len(CHUNKS) - 1 else nc.scalar.copy
+            copy(
+                res_il[:].rearrange("p (c i t) -> p c t i", i=4, t=PACK),
+                res[:].rearrange("p t (c i) -> p c t i", i=4),
+            )
+            nc.vector.quantize_mx(out=out_w[:, cols].bitcast(FP8X4), scales=out_sc[:, cols], in_=res_il[:])
+            nc.sync.dma_start(words_of(out_1)[:, cols], out_w[:, cols].bitcast(I32))
+            c0 += width
+        for q in range(4):
+            queue = nc.scalar if q % 2 else nc.sync
+            queue.dma_start(out_2[0, 4 * q : 4 * q + 4, :].bitcast(I32), out_sc[32 * q : 32 * q + 4, :].bitcast(I32))

@@ -86,7 +86,7 @@ def tile_picked_kqstdtwicpkind_none_po_kernel(
         tab_rows = tab.rearrange("(p t) j -> p t j", t=PACK)
         tab_t = []
         for t in range(PACK):
-            tab_t.append(held([P, N], F32, "tab%d" % t))
+            tab_t.append(held([P, 2 * N], F32, "tab%d" % t))
             nc.sync.dma_start(tab_t[t][:, 0:N], tab_rows[:, t, :])
 
         ident = held([P, P], F32, "ident")
@@ -139,6 +139,8 @@ def tile_picked_kqstdtwicpkind_none_po_kernel(
             a_win.append(held([P, 2 * N], F32, "a_win%d" % t))
             nc.scalar.copy(a_win[t][:, 0:N], acc[:])
             nc.scalar.activation(a_win[t][:, N : 2 * N], acc[:], ACT.Copy, scale=5.0 / 3.0)
+            neg_win.append(held([P, 2 * N], F32, "neg_win%d" % t))
+            nc.scalar.activation(neg_win[t][:, 0:N], acc[:], ACT.Copy, scale=-1.0)
         for t in range(PACK):
             acc = product(w2_d, w_sc, 4, t, xb_w, xb_sc)
             b_win.append(held([P, 2 * N], F32, "b_win%d" % t))
@@ -165,9 +167,7 @@ def tile_picked_kqstdtwicpkind_none_po_kernel(
             pa = ring.tile([P, N], F32, name="pa")
             neg_sum = ring.tile([P, N], F32, name="neg_sum")
             nc.vector.tensor_copy(pa[:], a_win[t][:].indirect(n1_t[:]))
-            pb = ring.tile([P, N], F32, name="pb")
-            nc.vector.tensor_copy(pb[:], a_win[t][:].indirect(n2_t[:]))
-            nc.vector.scalar_tensor_tensor(neg_sum[:], pa[:], -1.0, pb[:], ALU.mult, ALU.subtract)
+            nc.vector.tensor_tensor(neg_sum[:], neg_win[t][:].indirect(n2_t[:]), pa[:], ALU.subtract)
             centred.append(held([P, N], F32, "centred%d" % t))
             nc.vector.scalar_tensor_tensor(centred[t][:], a, 2.2, neg_sum[:], ALU.mult, ALU.add)
             diff = turned_sum([pa[:], pa[:], neg_sum[:]])
@@ -212,11 +212,6 @@ def tile_picked_kqstdtwicpkind_none_po_kernel(
         )
         z_w = held([P, N], U32, "z_w")
         z_sc = held([P, N], U8, "z_sc")
-        for t in range(PACK):
-            for h in range(2):
-                nc.vector.tensor_copy(
-                    looked[:, t, 256 * h : 256 * (h + 1)], tab_t[t][:].indirect(n4_t[:, 16 * h : 16 * (h + 1)])
-                )
         nc.vector.quantize_mx(out=z_w[:].bitcast(FP8X4), scales=z_sc[:], in_=z_il[:])
 
         s_win = []
@@ -225,7 +220,7 @@ def tile_picked_kqstdtwicpkind_none_po_kernel(
             acc = product(z_w, z_sc, 0, t, z2_w, z2_sc)
             s_win.append(held([P, N], F32, "s_win%d" % t))
             nc.scalar.activation(s_win[t][:], acc[:], ACT.Copy, scale=0.0625)
-            nc.vector.scalar_tensor_tensor(with_tab[:, t, :], acc[:], 0.0625, looked[:, t, :], ALU.mult, ALU.add)
+            nc.vector.tensor_tensor(with_tab[:, t, :], tab_t[t][:].indirect(n4_t[:]), s_win[t][:], ALU.add)
 
         out_rows = out_0.rearrange("(p t) v -> p t v", t=PACK)
         out_w = held([P, N], U32, "out_w")

@@ -29,11 +29,13 @@ def tile_picked_kqstdtwicpkind_none_po_kernel(
     nc = tc.nc
     with ExitStack() as ctx:
         keep = ctx.enter_context(tc.tile_pool(name="keep", bufs=1))
-        ring = ctx.enter_context(tc.tile_pool(name="ring", bufs=2))
         psum = ctx.enter_context(tc.psum_pool(name="psum", bufs=8))
 
         def held(shape, dtype, name):
             return keep.tile(shape, dtype, name=name, align_bytes=64)
+
+        def four(shape, dtype, name):
+            return [held(shape, dtype, "%s%d" % (name, t)) for t in range(PACK)]
 
         def bank():
             return psum.tile([P, N], F32, name="bank")
@@ -46,36 +48,39 @@ def tile_picked_kqstdtwicpkind_none_po_kernel(
         def words_of(src):
             return src[0].rearrange("p n r -> p (n r)").bitcast(I32)
 
-        def load_scale_rows(tile, first, src, quadrants):
+        def load_words(src, width, name):
+            tile = held([P, width], U32, name)
+            nc.sync.dma_start(tile[:].bitcast(I32), words_of(src))
+            return tile
+
+        def load_scale_rows(queue, tile, first, src, quadrants):
             for q in quadrants:
-                nc.sync.dma_start(
+                queue.dma_start(
                     tile[32 * q + first : 32 * q + first + 4, :].bitcast(I32),
                     src[0, 4 * q : 4 * q + 4, :].bitcast(I32),
                 )
 
         x_sc = held([P, T], U8, "x_sc")
-        w_sc_raw = held([P, N], U8, "w_sc_raw")
+        w1_sc_raw = held([P, N], U8, "w1_sc_raw")
+        w2_sc_raw = held([P, N], U8, "w2_sc_raw")
         nc.gpsimd.memset(x_sc[:].bitcast(I32), 0)
-        nc.gpsimd.memset(w_sc_raw[:].bitcast(I32), 0)
+        nc.gpsimd.memset(w1_sc_raw[:].bitcast(I32), 0)
+        nc.gpsimd.memset(w2_sc_raw[:].bitcast(I32), 0)
         warm = held([P, 1], F32, "warm")
         nc.vector.memset(warm[:], 0.0)
         warm_out = held([P, 1], F32, "warm_out")
         nc.scalar.activation(warm_out[:], warm[:], ACT.Sigmoid)
 
-        load_scale_rows(x_sc, 0, x_scales, range(4))
+        w1_raw = load_words(w1_words, N, "w1_raw")
+        load_scale_rows(nc.sync, x_sc, 0, x_scales, range(4))
         offs_t = load_list(offs, "offs_t")
-        load_scale_rows(w_sc_raw, 0, w1_scales, range(1))
-        w1_raw = held([P, N], U32, "w1_raw")
-        nc.sync.dma_start(w1_raw[:].bitcast(I32), words_of(w1_words))
-        x_w = held([P, T], U32, "x_w")
-        nc.sync.dma_start(x_w[:].bitcast(I32), words_of(x_words))
-        load_scale_rows(w_sc_raw, 0, w1_scales, range(1, 4))
-        load_scale_rows(w_sc_raw, 4, w2_scales, range(4))
         two_t = load_list(two, "two_t")
+        x_w = load_words(x_words, T, "x_w")
+        load_scale_rows(nc.sync, w1_sc_raw, 0, w1_scales, range(4))
         n1_t = load_list(n1, "n1_t")
         n2_t = load_list(n2, "n2_t")
-        w2_raw = held([P, N], U32, "w2_raw")
-        nc.sync.dma_start(w2_raw[:].bitcast(I32), words_of(w2_words))
+        w2_raw = load_words(w2_words, N, "w2_raw")
+        load_scale_rows(nc.sync, w2_sc_raw, 0, w2_scales, range(4))
         n3_t = load_list(n3, "n3_t")
         ga_t = held([P, PACK], F32, "ga_t")
         gb_t = held([P, PACK], F32, "gb_t")
@@ -84,28 +89,27 @@ def tile_picked_kqstdtwicpkind_none_po_kernel(
         n4_t = load_list(n4, "n4_t")
         n5_t = load_list(n5, "n5_t")
         tab_rows = tab.rearrange("(p t) j -> p t j", t=PACK)
-        tab_t = []
+        tab_win = four([P, 2 * N], F32, "tab_win")
         for t in range(PACK):
-            tab_t.append(held([P, 2 * N], F32, "tab%d" % t))
-            nc.sync.dma_start(tab_t[t][:, 0:N], tab_rows[:, t, :])
+            nc.sync.dma_start(tab_win[t][:, 0:N], tab_rows[:, t, :])
 
         ident = held([P, P], F32, "ident")
         make_identity(nc, ident[:])
 
+        twice = held([P, PACK], F32, "twice")
         sign = held([P, PACK], F32, "sign")
-        half = held([P, PACK], F32, "half")
+        sign_c = held([P, PACK], F32, "sign_c")
         gb_abs = held([P, PACK], F32, "gb_abs")
         ga_signed = held([P, PACK], F32, "ga_signed")
-        sign_c = held([P, PACK], F32, "sign_c")
-        nc.gpsimd.tensor_scalar(half[:], gb_t[:], 0.0, 2.0, ALU.is_ge, ALU.mult)
-        nc.gpsimd.tensor_scalar(sign[:], half[:], 1.0, -1.0, ALU.mult, ALU.add)
-        nc.gpsimd.tensor_scalar(sign_c[:], half[:], C, -C, ALU.mult, ALU.add)
+        nc.gpsimd.tensor_scalar(twice[:], gb_t[:], 0.0, 2.0, ALU.is_ge, ALU.mult)
+        nc.gpsimd.tensor_scalar(sign[:], twice[:], 1.0, -1.0, ALU.mult, ALU.add)
+        nc.gpsimd.tensor_scalar(sign_c[:], twice[:], C, -C, ALU.mult, ALU.add)
         nc.gpsimd.tensor_tensor(gb_abs[:], gb_t[:], sign[:], ALU.mult)
         nc.gpsimd.tensor_tensor(ga_signed[:], ga_t[:], sign_c[:], ALU.mult)
 
         def deal(dst, src):
-            nc.vector.tensor_copy(
-                dst.rearrange("p (t m) -> p m t", t=PACK), src.rearrange("p (m t) -> p m t", t=PACK)
+            nc.gpsimd.tensor_copy(
+                dst.rearrange("p (t m) -> p t m", t=PACK), src.rearrange("p (m t) -> p t m", t=PACK)
             )
 
         def pick(src, lst, dtype, name):
@@ -113,15 +117,17 @@ def tile_picked_kqstdtwicpkind_none_po_kernel(
             nc.vector.tensor_copy(tile[:], src[:].indirect(lst[:]))
             return tile
 
-        xa_sc = pick(x_sc, offs_t, U8, "xa_sc")
-        xb_sc = pick(x_sc, two_t, U8, "xb_sc")
         w1_d = held([P, N], U32, "w1_d")
         w2_d = held([P, N], U32, "w2_d")
-        w_sc = held([P, N], U8, "w_sc")
+        w1_sc = held([P, N], U8, "w1_sc")
+        w2_sc = held([P, N], U8, "w2_sc")
+        xa_sc = pick(x_sc, offs_t, U8, "xa_sc")
+        xb_sc = pick(x_sc, two_t, U8, "xb_sc")
         deal(w1_d[:].bitcast(I32), w1_raw[:].bitcast(I32))
-        deal(w_sc[:], w_sc_raw[:])
+        deal(w1_sc[:], w1_sc_raw[:])
         xa_w = pick(x_w, offs_t, U32, "xa_w")
         xb_w = pick(x_w, two_t, U32, "xb_w")
+        deal(w2_sc[:], w2_sc_raw[:])
         deal(w2_d[:].bitcast(I32), w2_raw[:].bitcast(I32))
 
         def product(lhs_w, lhs_sc, first, t, rhs_w, rhs_sc):
@@ -133,22 +139,23 @@ def tile_picked_kqstdtwicpkind_none_po_kernel(
             )
             return acc
 
-        a_win, b_win, neg_win = [], [], []
+        a_win = four([P, 2 * N], F32, "a_win")
+        neg_win = four([P, 2 * N], F32, "neg_win")
+        a_53 = four([P, N], F32, "a_53")
+        for pair in ((0, 1), (2, 3)):
+            accs = {t: product(w1_d, w1_sc, 0, t, xa_w, xa_sc) for t in pair}
+            for t in pair:
+                nc.scalar.copy(a_win[t][:, 0:N], accs[t][:])
+            for t in pair:
+                nc.scalar.activation(neg_win[t][:, 0:N], accs[t][:], ACT.Copy, scale=-1.0)
+            for t in pair:
+                nc.scalar.activation(a_53[t][:], accs[t][:], ACT.Copy, scale=5.0 / 3.0)
+        b_win = four([P, 2 * N], F32, "b_win")
+        gate = four([P, N], F32, "gate")
         for t in range(PACK):
-            acc = product(w1_d, w_sc, 0, t, xa_w, xa_sc)
-            a_win.append(held([P, 2 * N], F32, "a_win%d" % t))
-            nc.scalar.copy(a_win[t][:, 0:N], acc[:])
-            nc.scalar.activation(a_win[t][:, N : 2 * N], acc[:], ACT.Copy, scale=5.0 / 3.0)
-            neg_win.append(held([P, 2 * N], F32, "neg_win%d" % t))
-            nc.scalar.activation(neg_win[t][:, 0:N], acc[:], ACT.Copy, scale=-1.0)
-        for t in range(PACK):
-            acc = product(w2_d, w_sc, 4, t, xb_w, xb_sc)
-            b_win.append(held([P, 2 * N], F32, "b_win%d" % t))
+            acc = product(w2_d, w2_sc, 0, t, xb_w, xb_sc)
             nc.scalar.copy(b_win[t][:, 0:N], acc[:])
-        gates = []
-        for t in range(PACK):
-            gates.append(held([P, N], F32, "gate%d" % t))
-            nc.scalar.activation(gates[t][:], b_win[t][:].indirect(n3_t[:]), ACT.Sigmoid)
+            nc.scalar.activation(gate[t][:], b_win[t][:].indirect(n3_t[:]), ACT.Sigmoid)
 
         def turned_sum(terms):
             acc = bank()
@@ -161,44 +168,44 @@ def tile_picked_kqstdtwicpkind_none_po_kernel(
                     )
             return acc
 
-        centred, squares = [], []
+        pa = four([P, N], F32, "pa")
+        neg_sum = four([P, N], F32, "neg_sum")
+        centred = four([P, N], F32, "centred")
+        squares = four([P, 2, N], F32, "squares")
+        for pair in ((0, 1), (2, 3)):
+            for t in pair:
+                nc.vector.tensor_copy(pa[t][:], a_win[t][:].indirect(n1_t[:]))
+            for t in pair:
+                nc.vector.tensor_tensor(neg_sum[t][:], neg_win[t][:].indirect(n2_t[:]), pa[t][:], ALU.subtract)
+            for t in pair:
+                nc.vector.scalar_tensor_tensor(
+                    centred[t][:], a_win[t][:, 0:N], (1.0 - C) / C, neg_sum[t][:], ALU.mult, ALU.add
+                )
         for t in range(PACK):
-            a = a_win[t][:, 0:N]
-            pa = ring.tile([P, N], F32, name="pa")
-            neg_sum = ring.tile([P, N], F32, name="neg_sum")
-            nc.vector.tensor_copy(pa[:], a_win[t][:].indirect(n1_t[:]))
-            nc.vector.tensor_tensor(neg_sum[:], neg_win[t][:].indirect(n2_t[:]), pa[:], ALU.subtract)
-            centred.append(held([P, N], F32, "centred%d" % t))
-            nc.vector.scalar_tensor_tensor(centred[t][:], a, 2.2, neg_sum[:], ALU.mult, ALU.add)
-            diff = turned_sum([pa[:], pa[:], neg_sum[:]])
-            mean = turned_sum([neg_sum[:], a_win[t][:, N : 2 * N]])
-            sq = held([P, 2, N], F32, "sq%d" % t)
-            nc.scalar.activation(sq[:, 0, :], diff[:], ACT.Square)
-            nc.scalar.activation(sq[:, 1, :], mean[:], ACT.Square, scale=0.375)
-            squares.append(sq)
-        inv_root = []
+            diff = turned_sum([pa[t][:], pa[t][:], neg_sum[t][:]])
+            mean = turned_sum([neg_sum[t][:], a_53[t][:]])
+            nc.scalar.activation(squares[t][:, 0, :], diff[:], ACT.Square)
+            nc.scalar.activation(squares[t][:, 1, :], mean[:], ACT.Square, scale=0.375)
+        inv_root = four([P, N], F32, "inv_root")
         for t in range(PACK):
             total = turned_sum([squares[t][:, 0, :], squares[t][:, 1, :]])
-            inv_root.append(held([P, N], F32, "inv_root%d" % t))
             nc.scalar.activation(inv_root[t][:], total[:], ACT.Abs_reciprocal_sqrt, scale=0.5, bias=0.25)
 
-        looked = held([P, PACK, N], F32, "looked")
         z2_planes = held([P, PACK, N], BF16, "z2_planes")
-        for t in range(PACK):
-            st = a_win[t][:, 0:N]
-            nc.vector.scalar_tensor_tensor(
-                st, b_win[t][:, 0:N], gb_abs[:, t : t + 1], gates[t][:], ALU.mult, ALU.mult
-            )
-            nc.vector.tensor_copy(looked[:, t, :], a_win[t][:].indirect(n3_t[:]))
-            nc.vector.tensor_tensor(z2_planes[:, t, :], st, looked[:, t, :], ALU.max)
-        z2_il = held([P, N * PACK], BF16, "z2_il")
+        for pair in ((0, 1), (2, 3)):
+            for t in pair:
+                nc.vector.scalar_tensor_tensor(
+                    a_win[t][:, 0:N], b_win[t][:, 0:N], gb_abs[:, t : t + 1], gate[t][:], ALU.mult, ALU.mult
+                )
+            for t in pair:
+                nc.vector.tensor_copy(gate[t ^ 1][:], a_win[t][:].indirect(n3_t[:]))
+            for t in pair:
+                nc.vector.tensor_tensor(z2_planes[:, t, :], a_win[t][:, 0:N], gate[t ^ 1][:], ALU.max)
+        z2_il = squares[3][:].rearrange("p h n -> p (h n)").bitcast(BF16)
         nc.scalar.copy(
-            z2_il[:].rearrange("p (c i t) -> p c t i", i=4, t=PACK),
+            z2_il.rearrange("p (c i t) -> p c t i", i=4, t=PACK),
             z2_planes[:].rearrange("p t (c i) -> p c t i", i=4),
         )
-        z2_w = held([P, N], U32, "z2_w")
-        z2_sc = held([P, N], U8, "z2_sc")
-        nc.vector.quantize_mx(out=z2_w[:].bitcast(FP8X4), scales=z2_sc[:], in_=z2_il[:])
 
         z_planes = held([P, PACK, N], BF16, "z_planes")
         for t in range(PACK):
@@ -206,21 +213,27 @@ def tile_picked_kqstdtwicpkind_none_po_kernel(
                 z_planes[:, t, :], centred[t][:], ga_signed[:, t : t + 1], inv_root[t][:], ALU.mult, ALU.mult
             )
         z_il = held([P, N * PACK], BF16, "z_il")
-        nc.scalar.copy(
+        nc.vector.tensor_copy(
             z_il[:].rearrange("p (u m t) -> p m t u", u=PACK, t=PACK),
             z_planes[:].rearrange("p t (m u) -> p m t u", u=PACK),
         )
+        z2_w = held([P, N], U32, "z2_w")
+        z2_sc = held([P, N], U8, "z2_sc")
+        nc.vector.quantize_mx(out=z2_w[:].bitcast(FP8X4), scales=z2_sc[:], in_=z2_il)
         z_w = held([P, N], U32, "z_w")
         z_sc = held([P, N], U8, "z_sc")
-        nc.vector.quantize_mx(out=z_w[:].bitcast(FP8X4), scales=z_sc[:], in_=z_il[:])
+        for h in range(2):
+            cols = slice(256 * h, 256 * (h + 1))
+            nc.vector.quantize_mx(
+                out=z_w[:, cols].bitcast(FP8X4), scales=z_sc[:, cols], in_=z_il[:, 1024 * h : 1024 * (h + 1)]
+            )
 
-        s_win = []
+        s_win = four([P, N], F32, "s_win")
         with_tab = held([P, PACK, N], F32, "with_tab")
         for t in range(PACK):
             acc = product(z_w, z_sc, 0, t, z2_w, z2_sc)
-            s_win.append(held([P, N], F32, "s_win%d" % t))
             nc.scalar.activation(s_win[t][:], acc[:], ACT.Copy, scale=0.0625)
-            nc.vector.tensor_tensor(with_tab[:, t, :], tab_t[t][:].indirect(n4_t[:]), s_win[t][:], ALU.add)
+            nc.vector.tensor_tensor(with_tab[:, t, :], tab_win[t][:].indirect(n4_t[:]), s_win[t][:], ALU.add)
 
         out_rows = out_0.rearrange("(p t) v -> p t v", t=PACK)
         out_w = held([P, N], U32, "out_w")

@@ -17,9 +17,13 @@ P = 128
 PACK = 4
 T = 2048
 N = 512
+GROUP = 16
+LINE = 4
 C = 0.3125
-CHUNKS = (256, 128, 128)
-FLOPS = 3 * 2 * 512 * 512 * 512
+S_SCALE = 0.0625
+PAIRS = ((0, 1), (2, 3))
+CHUNKS = (slice(0, 256), slice(256, 384), slice(384, 512))
+FLOPS = 3 * 2 * N * N * N
 
 
 def tile_picked_kqstdtwicpkind_none_po_kernel(
@@ -34,53 +38,53 @@ def tile_picked_kqstdtwicpkind_none_po_kernel(
         def held(shape, dtype, name):
             return keep.tile(shape, dtype, name=name, align_bytes=64)
 
-        def four(shape, dtype, name):
+        def row_tiles(shape, dtype, name):
             return [held(shape, dtype, "%s%d" % (name, t)) for t in range(PACK)]
 
         def bank():
             return psum.tile([P, N], F32, name="bank")
 
         def load_list(src, name):
-            tile = keep.tile([P, N // 16], U16, name=name)
+            tile = keep.tile([P, N // GROUP], U16, name=name)
             nc.sync.dma_start(tile[:], src)
             return tile
 
-        def words_of(src):
-            return src[0].rearrange("p n r -> p (n r)").bitcast(I32)
+        def words_of(dram):
+            return dram[0].rearrange("p n r -> p (n r)").bitcast(I32)
+
+        def scale_rows(tile, dram, q):
+            return tile[32 * q : 32 * q + 4, :].bitcast(I32), dram[0, 4 * q : 4 * q + 4, :].bitcast(I32)
 
         def load_words(src, width, name):
             tile = held([P, width], U32, name)
             nc.sync.dma_start(tile[:].bitcast(I32), words_of(src))
             return tile
 
-        def load_scale_rows(queue, tile, first, src, quadrants):
-            for q in quadrants:
-                queue.dma_start(
-                    tile[32 * q + first : 32 * q + first + 4, :].bitcast(I32),
-                    src[0, 4 * q : 4 * q + 4, :].bitcast(I32),
-                )
+        def load_scales(tile, src):
+            for q in range(4):
+                nc.sync.dma_start(*scale_rows(tile, src, q))
 
         x_sc = held([P, T], U8, "x_sc")
         w1_sc_raw = held([P, N], U8, "w1_sc_raw")
         w2_sc_raw = held([P, N], U8, "w2_sc_raw")
-        nc.gpsimd.memset(x_sc[:].bitcast(I32), 0)
-        nc.gpsimd.memset(w1_sc_raw[:].bitcast(I32), 0)
-        nc.gpsimd.memset(w2_sc_raw[:].bitcast(I32), 0)
-        warm = held([P, 1], F32, "warm")
-        nc.vector.memset(warm[:], 0.0)
-        warm_out = held([P, 1], F32, "warm_out")
-        nc.scalar.activation(warm_out[:], warm[:], ACT.Sigmoid)
+        for tile in (x_sc, w1_sc_raw, w2_sc_raw):
+            nc.gpsimd.memset(tile[:].bitcast(I32), 0)
+
+        zero = held([P, 1], F32, "zero")
+        nc.vector.memset(zero[:], 0.0)
+        half = held([P, 1], F32, "half")
+        nc.scalar.activation(half[:], zero[:], ACT.Sigmoid)
 
         w1_raw = load_words(w1_words, N, "w1_raw")
-        load_scale_rows(nc.sync, x_sc, 0, x_scales, range(4))
+        load_scales(x_sc, x_scales)
         offs_t = load_list(offs, "offs_t")
         two_t = load_list(two, "two_t")
         x_w = load_words(x_words, T, "x_w")
-        load_scale_rows(nc.sync, w1_sc_raw, 0, w1_scales, range(4))
+        load_scales(w1_sc_raw, w1_scales)
         n1_t = load_list(n1, "n1_t")
         n2_t = load_list(n2, "n2_t")
         w2_raw = load_words(w2_words, N, "w2_raw")
-        load_scale_rows(nc.sync, w2_sc_raw, 0, w2_scales, range(4))
+        load_scales(w2_sc_raw, w2_scales)
         n3_t = load_list(n3, "n3_t")
         ga_t = held([P, PACK], F32, "ga_t")
         gb_t = held([P, PACK], F32, "gb_t")
@@ -89,7 +93,7 @@ def tile_picked_kqstdtwicpkind_none_po_kernel(
         n4_t = load_list(n4, "n4_t")
         n5_t = load_list(n5, "n5_t")
         tab_rows = tab.rearrange("(p t) j -> p t j", t=PACK)
-        tab_win = four([P, 2 * N], F32, "tab_win")
+        tab_win = row_tiles([P, 2 * N], F32, "tab_win")
         for t in range(PACK):
             nc.sync.dma_start(tab_win[t][:, 0:N], tab_rows[:, t, :])
 
@@ -107,55 +111,36 @@ def tile_picked_kqstdtwicpkind_none_po_kernel(
         nc.gpsimd.tensor_tensor(gb_abs[:], gb_t[:], sign[:], ALU.mult)
         nc.gpsimd.tensor_tensor(ga_signed[:], ga_t[:], sign_c[:], ALU.mult)
 
-        def deal(dst, src):
-            nc.gpsimd.tensor_copy(
-                dst.rearrange("p (t m) -> p t m", t=PACK), src.rearrange("p (m t) -> p t m", t=PACK)
-            )
-
-        def pick(src, lst, dtype, name):
+        def deal(src, dtype, view, name):
             tile = held([P, N], dtype, name)
-            nc.vector.tensor_copy(tile[:], src[:].indirect(lst[:]))
+            nc.gpsimd.tensor_copy(
+                tile[:].bitcast(view).rearrange("p (t m) -> p t m", t=PACK),
+                src[:].bitcast(view).rearrange("p (m t) -> p t m", t=PACK),
+            )
             return tile
 
-        w1_d = held([P, N], U32, "w1_d")
-        w2_d = held([P, N], U32, "w2_d")
-        w1_sc = held([P, N], U8, "w1_sc")
-        w2_sc = held([P, N], U8, "w2_sc")
+        def pick(src, offsets, dtype, name):
+            tile = held([P, N], dtype, name)
+            nc.vector.tensor_copy(tile[:], src[:].indirect(offsets[:]))
+            return tile
+
         xa_sc = pick(x_sc, offs_t, U8, "xa_sc")
         xb_sc = pick(x_sc, two_t, U8, "xb_sc")
-        deal(w1_d[:].bitcast(I32), w1_raw[:].bitcast(I32))
-        deal(w1_sc[:], w1_sc_raw[:])
+        w1_w = deal(w1_raw, U32, I32, "w1_w")
+        w1_sc = deal(w1_sc_raw, U8, U8, "w1_sc")
         xa_w = pick(x_w, offs_t, U32, "xa_w")
         xb_w = pick(x_w, two_t, U32, "xb_w")
-        deal(w2_sc[:], w2_sc_raw[:])
-        deal(w2_d[:].bitcast(I32), w2_raw[:].bitcast(I32))
+        w2_sc = deal(w2_sc_raw, U8, U8, "w2_sc")
+        w2_w = deal(w2_raw, U32, I32, "w2_w")
 
-        def product(lhs_w, lhs_sc, first, t, rhs_w, rhs_sc):
+        def product(lhs_w, lhs_sc, t, rhs_w, rhs_sc):
             acc = bank()
             cols = slice(P * t, P * (t + 1))
             nc.tensor.matmul_mx(
-                out=acc[:], lhsT=lhs_w[:, cols].bitcast(FP8X4), lhsT_scale=lhs_sc[first:P, cols],
+                out=acc[:], lhsT=lhs_w[:, cols].bitcast(FP8X4), lhsT_scale=lhs_sc[:, cols],
                 rhs=rhs_w[:].bitcast(FP8X4), rhs_scale=rhs_sc[:], start=True, stop=True,
             )
             return acc
-
-        a_win = four([P, 2 * N], F32, "a_win")
-        neg_win = four([P, 2 * N], F32, "neg_win")
-        a_53 = four([P, N], F32, "a_53")
-        for pair in ((0, 1), (2, 3)):
-            accs = {t: product(w1_d, w1_sc, 0, t, xa_w, xa_sc) for t in pair}
-            for t in pair:
-                nc.scalar.copy(a_win[t][:, 0:N], accs[t][:])
-            for t in pair:
-                nc.scalar.activation(neg_win[t][:, 0:N], accs[t][:], ACT.Copy, scale=-1.0)
-            for t in pair:
-                nc.scalar.activation(a_53[t][:], accs[t][:], ACT.Copy, scale=5.0 / 3.0)
-        b_win = four([P, 2 * N], F32, "b_win")
-        gate = four([P, N], F32, "gate")
-        for t in range(PACK):
-            acc = product(w2_d, w2_sc, 0, t, xb_w, xb_sc)
-            nc.scalar.copy(b_win[t][:, 0:N], acc[:])
-            nc.scalar.activation(gate[t][:], b_win[t][:].indirect(n3_t[:]), ACT.Sigmoid)
 
         def turned_sum(terms):
             acc = bank()
@@ -168,11 +153,35 @@ def tile_picked_kqstdtwicpkind_none_po_kernel(
                     )
             return acc
 
-        pa = four([P, N], F32, "pa")
-        neg_sum = four([P, N], F32, "neg_sum")
-        centred = four([P, N], F32, "centred")
-        squares = four([P, 2, N], F32, "squares")
-        for pair in ((0, 1), (2, 3)):
+        def interleave(copy, dst, planes):
+            copy(
+                dst.rearrange("p (c i t) -> p c t i", i=LINE, t=PACK),
+                planes.rearrange("p t (c i) -> p c t i", i=LINE),
+            )
+
+        a_win = row_tiles([P, 2 * N], F32, "a_win")
+        neg_win = row_tiles([P, 2 * N], F32, "neg_win")
+        a_scaled = row_tiles([P, N], F32, "a_scaled")
+        for pair in PAIRS:
+            accs = {t: product(w1_w, w1_sc, t, xa_w, xa_sc) for t in pair}
+            for t in pair:
+                nc.scalar.copy(a_win[t][:, 0:N], accs[t][:])
+            for t in pair:
+                nc.scalar.activation(neg_win[t][:, 0:N], accs[t][:], ACT.Copy, scale=-1.0)
+            for t in pair:
+                nc.scalar.activation(a_scaled[t][:], accs[t][:], ACT.Copy, scale=2.0 * C / (1.0 - 2.0 * C))
+        b_win = row_tiles([P, 2 * N], F32, "b_win")
+        gate = row_tiles([P, N], F32, "gate")
+        for t in range(PACK):
+            acc = product(w2_w, w2_sc, t, xb_w, xb_sc)
+            nc.scalar.copy(b_win[t][:, 0:N], acc[:])
+            nc.scalar.activation(gate[t][:], b_win[t][:].indirect(n3_t[:]), ACT.Sigmoid)
+
+        pa = row_tiles([P, N], F32, "pa")
+        neg_sum = row_tiles([P, N], F32, "neg_sum")
+        centred = row_tiles([P, N], F32, "centred")
+        squares = row_tiles([P, 2, N], F32, "squares")
+        for pair in PAIRS:
             for t in pair:
                 nc.vector.tensor_copy(pa[t][:], a_win[t][:].indirect(n1_t[:]))
             for t in pair:
@@ -182,80 +191,80 @@ def tile_picked_kqstdtwicpkind_none_po_kernel(
                     centred[t][:], a_win[t][:, 0:N], (1.0 - C) / C, neg_sum[t][:], ALU.mult, ALU.add
                 )
         for t in range(PACK):
-            diff = turned_sum([pa[t][:], pa[t][:], neg_sum[t][:]])
-            mean = turned_sum([neg_sum[t][:], a_53[t][:]])
-            nc.scalar.activation(squares[t][:, 0, :], diff[:], ACT.Square)
-            nc.scalar.activation(squares[t][:, 1, :], mean[:], ACT.Square, scale=0.375)
-        inv_root = four([P, N], F32, "inv_root")
+            difference = turned_sum([pa[t][:], pa[t][:], neg_sum[t][:]])
+            common = turned_sum([neg_sum[t][:], a_scaled[t][:]])
+            nc.scalar.activation(squares[t][:, 0, :], difference[:], ACT.Square)
+            nc.scalar.activation(squares[t][:, 1, :], common[:], ACT.Square, scale=1.0 - 2.0 * C)
+        inv_root = row_tiles([P, N], F32, "inv_root")
         for t in range(PACK):
             total = turned_sum([squares[t][:, 0, :], squares[t][:, 1, :]])
-            nc.scalar.activation(inv_root[t][:], total[:], ACT.Abs_reciprocal_sqrt, scale=0.5, bias=0.25)
+            nc.scalar.activation(inv_root[t][:], total[:], ACT.Abs_reciprocal_sqrt, scale=half[:], bias=0.25)
 
+        st_win = a_win
         z2_planes = held([P, PACK, N], BF16, "z2_planes")
-        for pair in ((0, 1), (2, 3)):
+        for pair in PAIRS:
             for t in pair:
                 nc.vector.scalar_tensor_tensor(
-                    a_win[t][:, 0:N], b_win[t][:, 0:N], gb_abs[:, t : t + 1], gate[t][:], ALU.mult, ALU.mult
+                    st_win[t][:, 0:N], b_win[t][:, 0:N], gb_abs[:, t : t + 1], gate[t][:], ALU.mult, ALU.mult
                 )
+            st_looked = {t: gate[t ^ 1] for t in pair}
             for t in pair:
-                nc.vector.tensor_copy(gate[t ^ 1][:], a_win[t][:].indirect(n3_t[:]))
+                nc.vector.tensor_copy(st_looked[t][:], st_win[t][:].indirect(n3_t[:]))
             for t in pair:
-                nc.vector.tensor_tensor(z2_planes[:, t, :], a_win[t][:, 0:N], gate[t ^ 1][:], ALU.max)
-        z2_il = squares[3][:].rearrange("p h n -> p (h n)").bitcast(BF16)
-        nc.scalar.copy(
-            z2_il.rearrange("p (c i t) -> p c t i", i=4, t=PACK),
-            z2_planes[:].rearrange("p t (c i) -> p c t i", i=4),
-        )
+                nc.vector.tensor_tensor(z2_planes[:, t, :], st_win[t][:, 0:N], st_looked[t][:], ALU.max)
+        z2_il = squares[PACK - 1][:].rearrange("p h n -> p (h n)").bitcast(BF16)
+        interleave(nc.scalar.copy, z2_il, z2_planes[:])
 
         z_planes = held([P, PACK, N], BF16, "z_planes")
         for t in range(PACK):
             nc.vector.scalar_tensor_tensor(
                 z_planes[:, t, :], centred[t][:], ga_signed[:, t : t + 1], inv_root[t][:], ALU.mult, ALU.mult
             )
-        z_il = held([P, N * PACK], BF16, "z_il")
-        nc.vector.tensor_copy(
-            z_il[:].rearrange("p (u m t) -> p m t u", u=PACK, t=PACK),
-            z_planes[:].rearrange("p t (m u) -> p m t u", u=PACK),
-        )
+        z_dealt = z_planes[:].rearrange("p t (m u) -> p m t u", u=PACK)
+        z_il = [held([P, 2 * P * PACK], BF16, "z_il%d" % h) for h in range(2)]
+        for h, copy in enumerate((nc.vector.tensor_copy, nc.scalar.copy)):
+            copy(z_il[h][:].rearrange("p (u m t) -> p m t u", u=2, t=PACK), z_dealt[:, :, :, 2 * h : 2 * h + 2])
         z2_w = held([P, N], U32, "z2_w")
         z2_sc = held([P, N], U8, "z2_sc")
         nc.vector.quantize_mx(out=z2_w[:].bitcast(FP8X4), scales=z2_sc[:], in_=z2_il)
         z_w = held([P, N], U32, "z_w")
         z_sc = held([P, N], U8, "z_sc")
         for h in range(2):
-            cols = slice(256 * h, 256 * (h + 1))
-            nc.vector.quantize_mx(
-                out=z_w[:, cols].bitcast(FP8X4), scales=z_sc[:, cols], in_=z_il[:, 1024 * h : 1024 * (h + 1)]
-            )
+            cols = slice(2 * P * h, 2 * P * (h + 1))
+            nc.vector.quantize_mx(out=z_w[:, cols].bitcast(FP8X4), scales=z_sc[:, cols], in_=z_il[h][:])
 
-        s_win = four([P, N], F32, "s_win")
+        tab_first = z_il[0][:].bitcast(F32)
+        nc.vector.tensor_copy(tab_first, tab_win[0][:].indirect(n4_t[:]))
+        s_win = row_tiles([P, N], F32, "s_win")
         with_tab = held([P, PACK, N], F32, "with_tab")
         for t in range(PACK):
-            acc = product(z_w, z_sc, 0, t, z2_w, z2_sc)
-            nc.scalar.activation(s_win[t][:], acc[:], ACT.Copy, scale=0.0625)
+            acc = product(z_w, z_sc, t, z2_w, z2_sc)
+            nc.scalar.activation(s_win[t][:], acc[:], ACT.Copy, scale=S_SCALE)
+        nc.vector.tensor_tensor(with_tab[:, 0, :], tab_first, s_win[0][:], ALU.add)
+        for t in range(1, PACK):
             nc.vector.tensor_tensor(with_tab[:, t, :], tab_win[t][:].indirect(n4_t[:]), s_win[t][:], ALU.add)
 
         out_rows = out_0.rearrange("(p t) v -> p t v", t=PACK)
         out_w = held([P, N], U32, "out_w")
         out_sc = held([P, N], U8, "out_sc")
-        c0 = 0
-        for k, width in enumerate(CHUNKS):
-            cols = slice(c0, c0 + width)
-            other = held([P, PACK, width], F32, "other%d" % k)
+        for k, cols in enumerate(CHUNKS):
+            width = cols.stop - cols.start
+            last = k == len(CHUNKS) - 1
+            s_looked = held([P, PACK, width], F32, "s_looked%d" % k)
             for t in range(PACK):
-                nc.vector.tensor_copy(other[:, t, :], s_win[t][:].indirect(n5_t[:, c0 // 16 : (c0 + width) // 16]))
+                offsets = n5_t[:, cols.start // GROUP : cols.stop // GROUP]
+                nc.vector.tensor_copy(s_looked[:, t, :], s_win[t][:].indirect(offsets))
             res = held([P, PACK, width], F32, "res%d" % k)
-            nc.vector.tensor_tensor(res[:], with_tab[:, :, cols], other[:], ALU.max)
+            for first, second in PAIRS:
+                rows = slice(first, second + 1)
+                nc.vector.tensor_tensor(res[:, rows, :], with_tab[:, rows, cols], s_looked[:, rows, :], ALU.max)
             nc.sync.dma_start(out_rows[:, :, cols], res[:])
             res_il = held([P, width * PACK], BF16, "res_il%d" % k)
-            copy = nc.vector.tensor_copy if k == len(CHUNKS) - 1 else nc.scalar.copy
-            copy(
-                res_il[:].rearrange("p (c i t) -> p c t i", i=4, t=PACK),
-                res[:].rearrange("p t (c i) -> p c t i", i=4),
-            )
+            interleave(nc.vector.tensor_copy if last else nc.scalar.copy, res_il[:], res[:])
             nc.vector.quantize_mx(out=out_w[:, cols].bitcast(FP8X4), scales=out_sc[:, cols], in_=res_il[:])
-            nc.sync.dma_start(words_of(out_1)[:, cols], out_w[:, cols].bitcast(I32))
-            c0 += width
+            queue = nc.sync if last else nc.scalar
+            queue.dma_start(words_of(out_1)[:, cols], out_w[:, cols].bitcast(I32))
         for q in range(4):
+            in_sbuf, in_hbm = scale_rows(out_sc, out_2, q)
             queue = nc.scalar if q % 2 else nc.sync
-            queue.dma_start(out_2[0, 4 * q : 4 * q + 4, :].bitcast(I32), out_sc[32 * q : 32 * q + 4, :].bitcast(I32))
+            queue.dma_start(in_hbm, in_sbuf)

from contextlib import ExitStack

import concourse.mybir as mybir
from concourse.masks import make_identity

F32 = mybir.dt.float32
BF16 = mybir.dt.bfloat16
I32 = mybir.dt.int32
U32 = mybir.dt.uint32
U16 = mybir.dt.uint16
U8 = mybir.dt.uint8
FP8X4 = mybir.dt.float8_e4m3fn_x4
ALU = mybir.AluOpType
ACT = mybir.ActivationFunctionType

P = 128
PACK = 4
T = 2048
N = 512
GROUP = 16
LINE = 4
C = 0.3125
S_SCALE = 0.0625
PAIRS = ((0, 1), (2, 3))
CHUNKS = (slice(0, 256), slice(256, 384), slice(384, 512))
FLOPS = 3 * 2 * N * N * N


def tile_picked_kqstdtwicpkind_none_po_kernel(
    tc, x_words, x_scales, w1_words, w1_scales, w2_words, w2_scales, ga, gb, tab,
    offs, two, n1, n2, n3, n4, n5, out_0, out_1, out_2,
):
    nc = tc.nc
    with ExitStack() as ctx:
        keep = ctx.enter_context(tc.tile_pool(name="keep", bufs=1))
        psum = ctx.enter_context(tc.psum_pool(name="psum", bufs=8))

        def held(shape, dtype, name):
            return keep.tile(shape, dtype, name=name, align_bytes=64)

        def row_tiles(shape, dtype, name):
            return [held(shape, dtype, "%s%d" % (name, t)) for t in range(PACK)]

        def bank():
            return psum.tile([P, N], F32, name="bank")

        def load_list(src, name):
            tile = keep.tile([P, N // GROUP], U16, name=name)
            nc.sync.dma_start(tile[:], src)
            return tile

        def words_of(dram):
            return dram[0].rearrange("p n r -> p (n r)").bitcast(I32)

        def scale_rows(tile, dram, q):
            return tile[32 * q : 32 * q + 4, :].bitcast(I32), dram[0, 4 * q : 4 * q + 4, :].bitcast(I32)

        def load_words(src, width, name):
            tile = held([P, width], U32, name)
            nc.sync.dma_start(tile[:].bitcast(I32), words_of(src))
            return tile

        def load_scales(tile, src):
            for q in range(4):
                nc.sync.dma_start(*scale_rows(tile, src, q))

        x_sc = held([P, T], U8, "x_sc")
        w1_sc_raw = held([P, N], U8, "w1_sc_raw")
        w2_sc_raw = held([P, N], U8, "w2_sc_raw")
        for tile in (x_sc, w1_sc_raw, w2_sc_raw):
            nc.gpsimd.memset(tile[:].bitcast(I32), 0)

        zero = held([P, 1], F32, "zero")
        nc.vector.memset(zero[:], 0.0)
        half = held([P, 1], F32, "half")
        nc.scalar.activation(half[:], zero[:], ACT.Sigmoid)

        w1_raw = load_words(w1_words, N, "w1_raw")
        load_scales(x_sc, x_scales)
        offs_t = load_list(offs, "offs_t")
        two_t = load_list(two, "two_t")
        x_w = load_words(x_words, T, "x_w")
        load_scales(w1_sc_raw, w1_scales)
        n1_t = load_list(n1, "n1_t")
        n2_t = load_list(n2, "n2_t")
        w2_raw = load_words(w2_words, N, "w2_raw")
        load_scales(w2_sc_raw, w2_scales)
        n3_t = load_list(n3, "n3_t")
        ga_t = held([P, PACK], F32, "ga_t")
        gb_t = held([P, PACK], F32, "gb_t")
        nc.sync.dma_start(ga_t[:], ga.rearrange("(p t) o -> p (t o)", t=PACK))
        nc.sync.dma_start(gb_t[:], gb.rearrange("(p t) o -> p (t o)", t=PACK))
        n4_t = load_list(n4, "n4_t")
        n5_t = load_list(n5, "n5_t")
        tab_rows = tab.rearrange("(p t) j -> p t j", t=PACK)
        tab_win = row_tiles([P, 2 * N], F32, "tab_win")
        for t in range(PACK):
            nc.sync.dma_start(tab_win[t][:, 0:N], tab_rows[:, t, :])

        ident = held([P, P], F32, "ident")
        make_identity(nc, ident[:])

        twice = held([P, PACK], F32, "twice")
        sign = held([P, PACK], F32, "sign")
        sign_c = held([P, PACK], F32, "sign_c")
        gb_abs = held([P, PACK], F32, "gb_abs")
        ga_signed = held([P, PACK], F32, "ga_signed")
        nc.gpsimd.tensor_scalar(twice[:], gb_t[:], 0.0, 2.0, ALU.is_ge, ALU.mult)
        nc.gpsimd.tensor_scalar(sign[:], twice[:], 1.0, -1.0, ALU.mult, ALU.add)
        nc.gpsimd.tensor_scalar(sign_c[:], twice[:], C, -C, ALU.mult, ALU.add)
        nc.gpsimd.tensor_tensor(gb_abs[:], gb_t[:], sign[:], ALU.mult)
        nc.gpsimd.tensor_tensor(ga_signed[:], ga_t[:], sign_c[:], ALU.mult)

        def deal(src, dtype, view, name):
            tile = held([P, N], dtype, name)
            nc.gpsimd.tensor_copy(
                tile[:].bitcast(view).rearrange("p (t m) -> p t m", t=PACK),
                src[:].bitcast(view).rearrange("p (m t) -> p t m", t=PACK),
            )
            return tile

        def pick(src, offsets, dtype, name):
            tile = held([P, N], dtype, name)
            nc.vector.tensor_copy(tile[:], src[:].indirect(offsets[:]))
            return tile

        xa_sc = pick(x_sc, offs_t, U8, "xa_sc")
        xb_sc = pick(x_sc, two_t, U8, "xb_sc")
        w1_w = deal(w1_raw, U32, I32, "w1_w")
        w1_sc = deal(w1_sc_raw, U8, U8, "w1_sc")
        xa_w = pick(x_w, offs_t, U32, "xa_w")
        xb_w = pick(x_w, two_t, U32, "xb_w")
        w2_sc = deal(w2_sc_raw, U8, U8, "w2_sc")
        w2_w = deal(w2_raw, U32, I32, "w2_w")

        def product(lhs_w, lhs_sc, t, rhs_w, rhs_sc):
            acc = bank()
            cols = slice(P * t, P * (t + 1))
            nc.tensor.matmul_mx(
                out=acc[:], lhsT=lhs_w[:, cols].bitcast(FP8X4), lhsT_scale=lhs_sc[:, cols],
                rhs=rhs_w[:].bitcast(FP8X4), rhs_scale=rhs_sc[:], start=True, stop=True,
            )
            return acc

        def turned_sum(terms):
            acc = bank()
            for k in range(N // P):
                cols = slice(P * k, P * (k + 1))
                for i, term in enumerate(terms):
                    nc.tensor.matmul(
                        acc[:, cols], lhsT=term[:, cols], rhs=ident[:], is_transpose=True,
                        start=(i == 0), stop=(i == len(terms) - 1),
                    )
            return acc

        def interleave(copy, dst, planes):
            copy(
                dst.rearrange("p (c i t) -> p c t i", i=LINE, t=PACK),
                planes.rearrange("p t (c i) -> p c t i", i=LINE),
            )

        a_win = row_tiles([P, 2 * N], F32, "a_win")
        neg_win = row_tiles([P, 2 * N], F32, "neg_win")
        a_scaled = row_tiles([P, N], F32, "a_scaled")
        for pair in PAIRS:
            accs = {t: product(w1_w, w1_sc, t, xa_w, xa_sc) for t in pair}
            for t in pair:
                nc.scalar.copy(a_win[t][:, 0:N], accs[t][:])
            for t in pair:
                nc.scalar.activation(neg_win[t][:, 0:N], accs[t][:], ACT.Copy, scale=-1.0)
            for t in pair:
                nc.scalar.activation(a_scaled[t][:], accs[t][:], ACT.Copy, scale=2.0 * C / (1.0 - 2.0 * C))
        b_win = row_tiles([P, 2 * N], F32, "b_win")
        gate = row_tiles([P, N], F32, "gate")
        for t in range(PACK):
            acc = product(w2_w, w2_sc, t, xb_w, xb_sc)
            nc.scalar.copy(b_win[t][:, 0:N], acc[:])
            nc.scalar.activation(gate[t][:], b_win[t][:].indirect(n3_t[:]), ACT.Sigmoid)

        pa = row_tiles([P, N], F32, "pa")
        neg_sum = row_tiles([P, N], F32, "neg_sum")
        centred = row_tiles([P, N], F32, "centred")
        squares = row_tiles([P, 2, N], F32, "squares")
        for pair in PAIRS:
            for t in pair:
                nc.vector.tensor_copy(pa[t][:], a_win[t][:].indirect(n1_t[:]))
            for t in pair:
                nc.vector.tensor_tensor(neg_sum[t][:], neg_win[t][:].indirect(n2_t[:]), pa[t][:], ALU.subtract)
            for t in pair:
                nc.vector.scalar_tensor_tensor(
                    centred[t][:], a_win[t][:, 0:N], (1.0 - C) / C, neg_sum[t][:], ALU.mult, ALU.add
                )
        for t in range(PACK):
            difference = turned_sum([pa[t][:], pa[t][:], neg_sum[t][:]])
            common = turned_sum([neg_sum[t][:], a_scaled[t][:]])
            nc.scalar.activation(squares[t][:, 0, :], difference[:], ACT.Square)
            nc.scalar.activation(squares[t][:, 1, :], common[:], ACT.Square, scale=1.0 - 2.0 * C)
        inv_root = row_tiles([P, N], F32, "inv_root")
        for t in range(PACK):
            total = turned_sum([squares[t][:, 0, :], squares[t][:, 1, :]])
            nc.scalar.activation(inv_root[t][:], total[:], ACT.Abs_reciprocal_sqrt, scale=half[:], bias=0.25)

        st_win = a_win
        z2_planes = held([P, PACK, N], BF16, "z2_planes")
        for pair in PAIRS:
            for t in pair:
                nc.vector.scalar_tensor_tensor(
                    st_win[t][:, 0:N], b_win[t][:, 0:N], gb_abs[:, t : t + 1], gate[t][:], ALU.mult, ALU.mult
                )
            st_looked = {t: gate[t ^ 1] for t in pair}
            for t in pair:
                nc.vector.tensor_copy(st_looked[t][:], st_win[t][:].indirect(n3_t[:]))
            for t in pair:
                nc.vector.tensor_tensor(z2_planes[:, t, :], st_win[t][:, 0:N], st_looked[t][:], ALU.max)
        z2_il = squares[PACK - 1][:].rearrange("p h n -> p (h n)").bitcast(BF16)
        interleave(nc.scalar.copy, z2_il, z2_planes[:])

        z_planes = held([P, PACK, N], BF16, "z_planes")
        for t in range(PACK):
            nc.vector.scalar_tensor_tensor(
                z_planes[:, t, :], centred[t][:], ga_signed[:, t : t + 1], inv_root[t][:], ALU.mult, ALU.mult
            )
        z_dealt = z_planes[:].rearrange("p t (m u) -> p m t u", u=PACK)
        z_il = [held([P, 2 * P * PACK], BF16, "z_il%d" % h) for h in range(2)]
        for h, copy in enumerate((nc.vector.tensor_copy, nc.scalar.copy)):
            copy(z_il[h][:].rearrange("p (u m t) -> p m t u", u=2, t=PACK), z_dealt[:, :, :, 2 * h : 2 * h + 2])
        z2_w = held([P, N], U32, "z2_w")
        z2_sc = held([P, N], U8, "z2_sc")
        nc.vector.quantize_mx(out=z2_w[:].bitcast(FP8X4), scales=z2_sc[:], in_=z2_il)
        z_w = held([P, N], U32, "z_w")
        z_sc = held([P, N], U8, "z_sc")
        for h in range(2):
            cols = slice(2 * P * h, 2 * P * (h + 1))
            nc.vector.quantize_mx(out=z_w[:, cols].bitcast(FP8X4), scales=z_sc[:, cols], in_=z_il[h][:])

        tab_first = z_il[0][:].bitcast(F32)
        nc.vector.tensor_copy(tab_first, tab_win[0][:].indirect(n4_t[:]))
        s_win = row_tiles([P, N], F32, "s_win")
        with_tab = held([P, PACK, N], F32, "with_tab")
        for t in range(PACK):
            acc = product(z_w, z_sc, t, z2_w, z2_sc)
            nc.scalar.activation(s_win[t][:], acc[:], ACT.Copy, scale=S_SCALE)
        nc.vector.tensor_tensor(with_tab[:, 0, :], tab_first, s_win[0][:], ALU.add)
        for t in range(1, PACK):
            nc.vector.tensor_tensor(with_tab[:, t, :], tab_win[t][:].indirect(n4_t[:]), s_win[t][:], ALU.add)

        out_rows = out_0.rearrange("(p t) v -> p t v", t=PACK)
        out_w = held([P, N], U32, "out_w")
        out_sc = held([P, N], U8, "out_sc")
        for k, cols in enumerate(CHUNKS):
            width = cols.stop - cols.start
            last = k == len(CHUNKS) - 1
            s_looked = held([P, PACK, width], F32, "s_looked%d" % k)
            for t in range(PACK):
                offsets = n5_t[:, cols.start // GROUP : cols.stop // GROUP]
                nc.vector.tensor_copy(s_looked[:, t, :], s_win[t][:].indirect(offsets))
            res = held([P, PACK, width], F32, "res%d" % k)
            for first, second in PAIRS:
                rows = slice(first, second + 1)
                nc.vector.tensor_tensor(res[:, rows, :], with_tab[:, rows, cols], s_looked[:, rows, :], ALU.max)
            nc.sync.dma_start(out_rows[:, :, cols], res[:])
            res_il = held([P, width * PACK], BF16, "res_il%d" % k)
            interleave(nc.vector.tensor_copy if last else nc.scalar.copy, res_il[:], res[:])
            nc.vector.quantize_mx(out=out_w[:, cols].bitcast(FP8X4), scales=out_sc[:, cols], in_=res_il[:])
            queue = nc.sync if last else nc.scalar
            queue.dma_start(words_of(out_1)[:, cols], out_w[:, cols].bitcast(I32))
        for q in range(4):
            in_sbuf, in_hbm = scale_rows(out_sc, out_2, q)
            queue = nc.scalar if q % 2 else nc.sync
            queue.dma_start(in_hbm, in_sbuf)
